import numpy as np
import ml_dtypes


def mxq(x, axis, fmt="e4m3"):
    dtype, down = {"e4m3": (ml_dtypes.float8_e4m3fn, 7), "e5m2": (ml_dtypes.float8_e5m2, 14)}[fmt]
    v = np.moveaxis(np.asarray(x, np.float32).astype(ml_dtypes.bfloat16).astype(np.float64), axis, -1)
    blocks = v.reshape(v.shape[:-1] + (-1, 32))
    amax = np.abs(blocks).max(-1, keepdims=True)
    byte = np.maximum(np.where(amax > 0, np.frexp(amax)[1] - 1 + 127, 0) - down, 1)
    scale = np.exp2(byte - 127.0)
    codes = (blocks / scale).astype(np.float32).astype(dtype).astype(np.float64)
    return np.moveaxis((codes * scale).reshape(v.shape), -1, axis)


WIDE = False


def mx_kscale(k):
    if not WIDE:
        return np.ones(k)
    levels = np.array([10, -10, 5, -5, 0])
    if k % 512:
        return np.exp2(np.random.permutation(np.resize(levels, k // 32))).repeat(32)
    a = np.empty((k // 512, 16))
    for p in range(k // 512):
        a[p, :8] = np.random.permutation(np.resize(levels, 8))
        for g in range(8):
            far = levels[np.abs(levels - a[p, g]) >= 10]
            a[p, g + 8] = far[np.random.randint(len(far))]
    return np.exp2(a.ravel()).repeat(32)


def f64(x):
    return np.asarray(x).astype(np.float64)


def striped(idx):
    return np.tile(idx.reshape(-1, 16).T, (8, 1)).astype(np.uint16)


def unstriped(offs):
    return offs[:16].T.reshape(-1).astype(np.int64)


def pack_weight(w):
    k, n = w.shape
    w = f64(np.asarray(w, np.float32).astype(ml_dtypes.bfloat16)).reshape(k // 32, 32, n)
    amax = np.abs(w).max(1)
    byte = np.clip(np.where(amax > 0, np.frexp(amax)[1] - 1 + 127 - 7, 1), 1, 254)
    scaled = (w * np.exp2(127.0 - byte)[:, None, :]).reshape(k, n).astype(np.float32)
    words = np.ascontiguousarray(scaled.reshape(k // 512, 128, 4, n).transpose(0, 1, 3, 2)).astype(ml_dtypes.float8_e4m3fn).view(np.uint8)
    return words, np.ascontiguousarray(byte.astype(np.uint8).reshape(k // 512, 16, n))


def unpack_weight(words, scales):
    g, p, n, _ = words.shape
    vals = np.ascontiguousarray(words).view(ml_dtypes.float8_e4m3fn).astype(np.float64) * np.repeat(np.exp2(scales.astype(np.float64) - 127.0), 8, axis=1)[..., None]
    return vals.transpose(0, 1, 3, 2).reshape(g * 512, n)


def gelu(v):
    return 0.5 * v * (1.0 + np.tanh(np.sqrt(2.0 / np.pi) * (v + 0.044715 * v**3)))


K, T, D, S, V, H, N = 1024, 2048, 4, 768, 384, 512, 512


def setup_inputs():
    n = np.random.standard_normal
    s = mx_kscale(K)[:, None]
    u = mx_kscale(H)
    packed = pack_weight(n((K, T)) * s)
    return {
        "x_words": packed[0],
        "x_scales": packed[1],
        "w1": (n((K, H)) / np.sqrt(K) / s * u).astype(np.float32),
        "w2": (n((H, N)) / np.sqrt(H) / u[:, None]).astype(np.float32),
        "gate": np.tile(np.random.uniform(0.2, 1.0, (D, 1, V)) / np.sqrt(D), (1, N, 1)).astype(np.float32),
        "offs": striped(np.random.permutation(T)[:S]),
        "pos1": striped(np.random.permutation(S)[:V]),
        "pos2": striped(np.random.permutation(S)[:V]),
        "pos3": striped(np.random.permutation(S)[:V]),
        "pos4": striped(np.random.permutation(S)[:V]),
    }


def reference(x_words, x_scales, w1, w2, gate, offs, pos1, pos2, pos3, pos4):
    idx = unstriped(offs)
    xq = unpack_weight(x_words, x_scales)[:, idx]
    h = gelu(mxq(f64(w1), 0, "e4m3").T @ xq)
    y = mxq(f64(w2), 0, "e4m3").T @ mxq(h, 0, "e4m3")
    return sum(f64(gate[d]) * y[:, unstriped(p)] for d, p in enumerate((pos1, pos2, pos3, pos4)))

@@ -1,0 +1,247 @@
+from contextlib import ExitStack
+
+import concourse.mybir as mybir
+from concourse.masks import make_identity
+
+K, T, D, S, V, H, N = 1024, 2048, 4, 768, 384, 512, 512
+FLOPS = 2 * K * H * S + 2 * H * N * S
+BYTES = K * T + K * T // 32 + 4 * K * H + 4 * H * N + 4 * D * V + 2 * 8 * (S + D * V) + 4 * N * V
+
+F32 = mybir.dt.float32
+BF16 = mybir.dt.bfloat16
+I32 = mybir.dt.int32
+U32 = mybir.dt.uint32
+U16 = mybir.dt.uint16
+U8 = mybir.dt.uint8
+FP8X4 = mybir.dt.float8_e4m3fn_x4
+ACT = mybir.ActivationFunctionType
+ALU = mybir.AluOpType
+
+P = 128
+PACK = 4
+PASSES = K // (P * PACK)
+CHUNK = 128
+CHUNKS = S // CHUNK
+SLICE = 256
+BLOCKS = N // P
+VCH = V // P
+BANK = 512
+FUSED = 2
+
+
+def tile_picked_sub_mlp_gelu_sub_p_kernel(
+    tc, x_words, x_scales, w1, w2, gate, offs, pos1, pos2, pos3, pos4, out
+):
+    nc = tc.nc
+    with ExitStack() as ctx:
+        keep = ctx.enter_context(tc.tile_pool(name="keep", bufs=1))
+        ring = ctx.enter_context(tc.tile_pool(name="ring", bufs=6))
+        psum = ctx.enter_context(tc.psum_pool(name="psum", bufs=1))
+
+        def bank(i):
+            return psum.tile([P, BANK], F32, name="bank%d" % i, tag="bank%d" % i)
+
+        xs_all = keep.tile([P, T], U8, name="xs_all", align_bytes=64)
+        nc.gpsimd.memset(xs_all[:].bitcast(I32), 0)
+        gate_rows = keep.tile([P, V], F32, name="gate_rows")
+        nc.gpsimd.memset(gate_rows[:], 0.0)
+        warm = keep.tile([P, 1], F32, name="warm")
+        nc.gpsimd.memset(warm[:], 0.0)
+        warm2 = keep.tile([P, 1], F32, name="warm2")
+        nc.scalar.activation(warm2[:], warm[:], ACT.Gelu_apprx_tanh)
+        ident = keep.tile([P, P], F32, name="ident")
+        make_identity(nc, ident[:])
+
+        w1_raw = [keep.tile([P, PACK, H], F32, name="w1_raw%d" % o) for o in range(PASSES)]
+        xw_all = [keep.tile([P, T], I32, name="xw_all%d" % o, align_bytes=64) for o in range(PASSES)]
+        offs_sb = keep.tile([P, S // 16], U16, name="offs_sb")
+        for o in range(PASSES):
+            nc.sync.dma_start(
+                out=w1_raw[o][:], in_=w1[512 * o : 512 * (o + 1), :].rearrange("(p j) c -> p j c", j=PACK)
+            )
+            if o == 0:
+                nc.sync.dma_start(offs_sb[:], offs)
+                for q in range(4):
+                    nc.sync.dma_start(
+                        out=xs_all[32 * q : 32 * q + 4 * PASSES, :].bitcast(I32),
+                        in_=x_scales[:, 4 * q : 4 * q + 4, :].bitcast(I32),
+                    )
+            nc.sync.dma_start(out=xw_all[o][:], in_=x_words[o].rearrange("p c r -> p (c r)").bitcast(I32))
+        w2_raw = keep.tile([P, PACK, N], F32, name="w2_raw")
+        nc.sync.dma_start(out=w2_raw[:], in_=w2.rearrange("(p j) c -> p j c", j=PACK))
+        pos_sb = []
+        for d, pos in enumerate((pos1, pos2, pos3, pos4)):
+            t = keep.tile([P, V // 16], U16, name="pos_sb%d" % d)
+            nc.sync.dma_start(t[:], pos)
+            pos_sb.append(t)
+        nc.sync.dma_start(out=gate_rows[0:D, :], in_=gate[:, 0, :])
+        gate_last = keep.tile([P, V], F32, name="gate_last")
+        nc.sync.dma_start(out=gate_last[:], in_=gate[D - 1, N - P : N, :])
+
+        w1_codes = [keep.tile([P, H], U32, name="w1_codes%d" % o, align_bytes=64) for o in range(PASSES)]
+        w1_scale = [keep.tile([P, H], U8, name="w1_scale%d" % o, align_bytes=64) for o in range(PASSES)]
+
+        def w1_prepare(o):
+            halves = []
+            for u in range(2):
+                g = keep.tile([P, 2, P, PACK], BF16, name="w1_bf%d%d" % (o, u), align_bytes=64)
+                src = w1_raw[o][:].rearrange("p j (m t) -> p m j t", t=PACK)[:, :, :, 2 * u : 2 * u + 2]
+                dst = g[:].rearrange("p t m j -> p m j t")
+                if u == 0 or o == 0:
+                    nc.scalar.copy(dst, src)
+                else:
+                    nc.vector.tensor_copy(dst, src)
+                halves.append(g)
+            for u in ((0, 1), (1, 0))[o]:
+                cols = slice(2 * P * u, 2 * P * (u + 1))
+                nc.vector.quantize_mx(
+                    out=w1_codes[o][:, cols].bitcast(FP8X4),
+                    scales=w1_scale[o][:, cols],
+                    in_=halves[u][:].rearrange("p t m j -> p (t m j)"),
+                )
+
+        def gather_words(o):
+            slices = []
+            for s in range(S // SLICE):
+                g = keep.tile([P, SLICE], U32, name="xw%d_%d" % (o, s), align_bytes=64)
+                nc.vector.tensor_copy(
+                    g[:], xw_all[o][:].bitcast(U32).indirect(offs_sb[:, SLICE // 16 * s : SLICE // 16 * (s + 1)])
+                )
+                slices.append(g)
+            return slices
+
+        xs = keep.tile([P, S], U8, name="xs", align_bytes=64)
+        nc.vector.tensor_copy(xs[:], xs_all[:].indirect(offs_sb[:]))
+        w1_prepare(0)
+        xw0 = gather_words(0)
+
+        h_bank = [bank(c) for c in range(CHUNKS)]
+        for c in range(CHUNKS):
+            cols = slice(CHUNK * c, CHUNK * (c + 1))
+            s, r = divmod(CHUNK * c, SLICE)
+            for t in range(PACK):
+                nc.tensor.matmul_mx(
+                    out=h_bank[c][:, CHUNK * t : CHUNK * (t + 1)],
+                    lhsT=w1_codes[0][:, P * t : P * (t + 1)].bitcast(FP8X4),
+                    lhsT_scale=w1_scale[0][:, P * t : P * (t + 1)],
+                    rhs=xw0[s][:, r : r + CHUNK].bitcast(FP8X4),
+                    rhs_scale=xs[:, cols],
+                    start=(t == 0),
+                    stop=False,
+                )
+
+        w1_prepare(1)
+
+        xw1 = gather_words(1)
+
+        h_codes = keep.tile([P, S], U32, name="h_codes", align_bytes=64)
+        h_scale = keep.tile([P, S], U8, name="h_scale", align_bytes=64)
+        w2_codes = keep.tile([P, N], U32, name="w2_codes", align_bytes=64)
+        w2_scale = keep.tile([P, N], U8, name="w2_scale", align_bytes=64)
+
+        def w2_prepare(u):
+            cols = slice(2 * P * u, 2 * P * (u + 1))
+            g = keep.tile([P, 2 * P, PACK], BF16, name="w2_bf%d" % u, align_bytes=64)
+            nc.vector.tensor_copy(
+                g[:].rearrange("p (c i) j -> p c j i", i=4),
+                w2_raw[:, :, cols].rearrange("p j (c i) -> p c j i", i=4),
+            )
+            nc.vector.quantize_mx(
+                out=w2_codes[:, cols].bitcast(FP8X4),
+                scales=w2_scale[:, cols],
+                in_=g[:].rearrange("p c j -> p (c j)"),
+            )
+
+        for c in range(CHUNKS):
+            cols = slice(CHUNK * c, CHUNK * (c + 1))
+            s, r = divmod(CHUNK * c, SLICE)
+            for t in range(PACK):
+                nc.tensor.matmul_mx(
+                    out=h_bank[c][:, CHUNK * t : CHUNK * (t + 1)],
+                    lhsT=w1_codes[1][:, P * t : P * (t + 1)].bitcast(FP8X4),
+                    lhsT_scale=w1_scale[1][:, P * t : P * (t + 1)],
+                    rhs=xw1[s][:, r : r + CHUNK].bitcast(FP8X4),
+                    rhs_scale=xs[4:P, cols],
+                    start=False,
+                    stop=(t == PACK - 1),
+                )
+            h_bf = keep.tile([P, CHUNK, PACK], BF16, name="h_bf%d" % c, align_bytes=64)
+            nc.scalar.activation(
+                h_bf[:], h_bank[c][:].rearrange("p (t n) -> p n t", t=PACK), ACT.Gelu_apprx_tanh
+            )
+            nc.vector.quantize_mx(
+                out=h_codes[:, cols].bitcast(FP8X4),
+                scales=h_scale[:, cols],
+                in_=h_bf[:].rearrange("p n t -> p (n t)"),
+            )
+            if c in (1, 2):
+                w2_prepare(c - 1)
+
+        y = []
+        for b in range(BLOCKS):
+            yb = keep.tile([P, S], F32, name="y%d" % b)
+            for part, (lo, hi) in enumerate(((0, BANK), (BANK, S))):
+                yb_bank = bank((6 + 2 * b + part) % 8)
+                nc.tensor.matmul_mx(
+                    out=yb_bank[:, 0 : hi - lo],
+                    lhsT=w2_codes[:, P * b : P * (b + 1)].bitcast(FP8X4),
+                    lhsT_scale=w2_scale[:, P * b : P * (b + 1)],
+                    rhs=h_codes[:, lo:hi].bitcast(FP8X4),
+                    rhs_scale=h_scale[:, lo:hi],
+                    start=True,
+                    stop=True,
+                )
+                if b == 0 and part == 1:
+                    nc.vector.tensor_copy(yb[:, lo:hi], yb_bank[:, 0 : hi - lo])
+                else:
+                    nc.scalar.copy(yb[:, lo:hi], yb_bank[:, 0 : hi - lo])
+            y.append(yb)
+
+        gt_bank = bank(7)
+        for c in range(VCH):
+            nc.tensor.transpose(gt_bank[:, P * c : P * (c + 1)], gate_rows[:, P * c : P * (c + 1)], ident[:])
+        gate_t = keep.tile([P, VCH, D], F32, name="gate_t")
+        nc.scalar.copy(gate_t[:], gt_bank[:, 0:V].rearrange("p (c r) -> p c r", c=VCH)[:, :, 0:D])
+
+        turn_banks = ((6, 7), (0, 1))
+        out_bank = [bank(2 + b) for b in range(BLOCKS)]
+        last = D - 1
+        unit = 0
+        for pair in range(BLOCKS // 2):
+            blocks = (2 * pair, 2 * pair + 1)
+            turns = D if pair == 0 else D - 1
+            for d in range(turns):
+                lo_bank, hi_bank = (bank(i) for i in turn_banks[unit % 2])
+                turned = [lo_bank[:, 0 : 2 * P], lo_bank[:, 2 * P : 4 * P], hi_bank[:, 0 : 2 * P]]
+                unit = unit + 1
+                for i, b in enumerate(blocks):
+                    g = ring.tile([P, V], F32, name="picked")
+                    nc.vector.tensor_copy(g[:], y[b][:].indirect(pos_sb[d][:]))
+                    for c in range(VCH):
+                        nc.tensor.transpose(turned[c][:, P * i : P * (i + 1)], g[:, P * c : P * (c + 1)], ident[:])
+                for c in range(VCH):
+                    scaled = ring.tile([P, 2 * P], F32, name="scaled")
+                    nc.scalar.activation(scaled[:], turned[c], ACT.Copy, scale=gate_t[:, c, d : d + 1])
+                    for i, b in enumerate(blocks):
+                        nc.tensor.matmul(
+                            out_bank[b][:, P * c : P * (c + 1)],
+                            scaled[:, P * i : P * (i + 1)],
+                            ident[:],
+                            is_transpose=True,
+                            start=(d == 0 and c == 0),
+                            stop=(d == turns - 1 and c == VCH - 1),
+                        )
+            if pair == 0:
+                for b in blocks:
+                    res = keep.tile([P, V], F32, name="res%d" % b)
+                    nc.scalar.copy(res[:], out_bank[b][:, 0:V])
+                    nc.sync.dma_start(out=out[P * b : P * (b + 1), :], in_=res[:])
+
+        terms = {}
+        for b in range(BLOCKS - FUSED, BLOCKS):
+            terms[b] = ring.tile([P, V], F32, name="picked")
+            nc.vector.tensor_tensor(terms[b][:], y[b][:].indirect(pos_sb[last][:]), gate_last[:], ALU.mult)
+        for b in range(BLOCKS - FUSED, BLOCKS):
+            res = keep.tile([P, V], F32, name="res%d" % b)
+            nc.vector.tensor_tensor(res[:], out_bank[b][:, 0:V], terms[b][:], ALU.add)
+            nc.sync.dma_start(out=out[P * b : P * (b + 1), :], in_=res[:])

@@ -27,6 +27,10 @@ BLOCKS = N // P
 VCH = V // P
 BANK = 512
 FUSED = 2
+CUTS = (
+    ((0, 256, "slot_bf00"), (256, 768, "slot_bf01")),
+    ((0, 256, "slot_bf10"), (256, 512, "slot_xall0"), (512, 768, "slot_w1raw1")),
+)
 
 
 def tile_picked_sub_mlp_gelu_sub_p_kernel(
@@ -41,19 +45,25 @@ def tile_picked_sub_mlp_gelu_sub_p_kernel(
         def bank(i):
             return psum.tile([P, BANK], F32, name="bank%d" % i, tag="bank%d" % i)
 
-        xs_all = keep.tile([P, T], U8, name="xs_all", align_bytes=64)
+        def slot(shape, dtype, name, tag):
+            return keep.tile(shape, dtype, name=name, tag=tag, align_bytes=64)
+
+        xs_all = slot([P, T], U8, "xs_all", "slot_scales")
         nc.gpsimd.memset(xs_all[:].bitcast(I32), 0)
-        gate_rows = keep.tile([P, V], F32, name="gate_rows")
-        nc.gpsimd.memset(gate_rows[:], 0.0)
+        for q in range(4):
+            nc.gpsimd.dma_start(
+                out=xs_all[32 * q : 32 * q + 4 * PASSES, :].bitcast(I32),
+                in_=x_scales[:, 4 * q : 4 * q + 4, :].bitcast(I32),
+            )
         warm = keep.tile([P, 1], F32, name="warm")
-        nc.gpsimd.memset(warm[:], 0.0)
+        nc.vector.memset(warm[:], 0.0)
         warm2 = keep.tile([P, 1], F32, name="warm2")
         nc.scalar.activation(warm2[:], warm[:], ACT.Gelu_apprx_tanh)
         ident = keep.tile([P, P], F32, name="ident")
         make_identity(nc, ident[:])
 
-        w1_raw = [keep.tile([P, PACK, H], F32, name="w1_raw%d" % o) for o in range(PASSES)]
-        xw_all = [keep.tile([P, T], I32, name="xw_all%d" % o, align_bytes=64) for o in range(PASSES)]
+        w1_raw = [slot([P, PACK, H], F32, "w1_raw%d" % o, "slot_w1raw%d" % o) for o in range(PASSES)]
+        xw_all = [slot([P, T], I32, "xw_all%d" % o, "slot_xall%d" % o) for o in range(PASSES)]
         offs_sb = keep.tile([P, S // 16], U16, name="offs_sb")
         for o in range(PASSES):
             nc.sync.dma_start(
@@ -61,11 +71,6 @@ def tile_picked_sub_mlp_gelu_sub_p_kernel(
             )
             if o == 0:
                 nc.sync.dma_start(offs_sb[:], offs)
-                for q in range(4):
-                    nc.sync.dma_start(
-                        out=xs_all[32 * q : 32 * q + 4 * PASSES, :].bitcast(I32),
-                        in_=x_scales[:, 4 * q : 4 * q + 4, :].bitcast(I32),
-                    )
             nc.sync.dma_start(out=xw_all[o][:], in_=x_words[o].rearrange("p c r -> p (c r)").bitcast(I32))
         w2_raw = keep.tile([P, PACK, N], F32, name="w2_raw")
         nc.sync.dma_start(out=w2_raw[:], in_=w2.rearrange("(p j) c -> p j c", j=PACK))
@@ -74,17 +79,19 @@ def tile_picked_sub_mlp_gelu_sub_p_kernel(
             t = keep.tile([P, V // 16], U16, name="pos_sb%d" % d)
             nc.sync.dma_start(t[:], pos)
             pos_sb.append(t)
-        nc.sync.dma_start(out=gate_rows[0:D, :], in_=gate[:, 0, :])
-        gate_last = keep.tile([P, V], F32, name="gate_last")
-        nc.sync.dma_start(out=gate_last[:], in_=gate[D - 1, N - P : N, :])
+        gate_sb = []
+        for d in range(D):
+            t = keep.tile([P, V], F32, name="gate_sb%d" % d)
+            nc.sync.dma_start(out=t[:], in_=gate[d, 0:P, :])
+            gate_sb.append(t)
 
         w1_codes = [keep.tile([P, H], U32, name="w1_codes%d" % o, align_bytes=64) for o in range(PASSES)]
-        w1_scale = [keep.tile([P, H], U8, name="w1_scale%d" % o, align_bytes=64) for o in range(PASSES)]
 
         def w1_prepare(o):
             halves = []
             for u in range(2):
-                g = keep.tile([P, 2, P, PACK], BF16, name="w1_bf%d%d" % (o, u), align_bytes=64)
+                tag = "slot_xall0" if (o, u) == (1, 1) else "slot_bf%d%d" % (o, u)
+                g = slot([P, 2, P, PACK], BF16, "w1_bf%d%d" % (o, u), tag)
                 src = w1_raw[o][:].rearrange("p j (m t) -> p m j t", t=PACK)[:, :, :, 2 * u : 2 * u + 2]
                 dst = g[:].rearrange("p t m j -> p m j t")
                 if u == 0 or o == 0:
@@ -102,29 +109,28 @@ def tile_picked_sub_mlp_gelu_sub_p_kernel(
 
         def gather_words(o):
             slices = []
-            for s in range(S // SLICE):
-                g = keep.tile([P, SLICE], U32, name="xw%d_%d" % (o, s), align_bytes=64)
-                nc.vector.tensor_copy(
-                    g[:], xw_all[o][:].bitcast(U32).indirect(offs_sb[:, SLICE // 16 * s : SLICE // 16 * (s + 1)])
-                )
-                slices.append(g)
+            for s, (lo, hi, tag) in enumerate(CUTS[o]):
+                g = slot([P, hi - lo], U32, "xw%d_%d" % (o, s), tag)
+                nc.vector.tensor_copy(g[:], xw_all[o][:].bitcast(U32).indirect(offs_sb[:, lo // 16 : hi // 16]))
+                slices.extend(g[:, r : r + CHUNK] for r in range(0, hi - lo, CHUNK))
             return slices
 
         xs = keep.tile([P, S], U8, name="xs", align_bytes=64)
         nc.vector.tensor_copy(xs[:], xs_all[:].indirect(offs_sb[:]))
+        w1_scales = slot([P, PASSES * H], U8, "w1_scales", "slot_scales")
+        w1_scale = [w1_scales[:, H * o : H * (o + 1)] for o in range(PASSES)]
         w1_prepare(0)
         xw0 = gather_words(0)
 
         h_bank = [bank(c) for c in range(CHUNKS)]
         for c in range(CHUNKS):
             cols = slice(CHUNK * c, CHUNK * (c + 1))
-            s, r = divmod(CHUNK * c, SLICE)
             for t in range(PACK):
                 nc.tensor.matmul_mx(
                     out=h_bank[c][:, CHUNK * t : CHUNK * (t + 1)],
                     lhsT=w1_codes[0][:, P * t : P * (t + 1)].bitcast(FP8X4),
                     lhsT_scale=w1_scale[0][:, P * t : P * (t + 1)],
-                    rhs=xw0[s][:, r : r + CHUNK].bitcast(FP8X4),
+                    rhs=xw0[c].bitcast(FP8X4),
                     rhs_scale=xs[:, cols],
                     start=(t == 0),
                     stop=False,
@@ -141,7 +147,7 @@ def tile_picked_sub_mlp_gelu_sub_p_kernel(
 
         def w2_prepare(u):
             cols = slice(2 * P * u, 2 * P * (u + 1))
-            g = keep.tile([P, 2 * P, PACK], BF16, name="w2_bf%d" % u, align_bytes=64)
+            g = slot([P, 2 * P, PACK], BF16, "w2_bf%d" % u, ("slot_xall1", "slot_bf01")[u])
             nc.vector.tensor_copy(
                 g[:].rearrange("p (c i) j -> p c j i", i=4),
                 w2_raw[:, :, cols].rearrange("p j (c i) -> p c j i", i=4),
@@ -154,13 +160,12 @@ def tile_picked_sub_mlp_gelu_sub_p_kernel(
 
         for c in range(CHUNKS):
             cols = slice(CHUNK * c, CHUNK * (c + 1))
-            s, r = divmod(CHUNK * c, SLICE)
             for t in range(PACK):
                 nc.tensor.matmul_mx(
                     out=h_bank[c][:, CHUNK * t : CHUNK * (t + 1)],
                     lhsT=w1_codes[1][:, P * t : P * (t + 1)].bitcast(FP8X4),
                     lhsT_scale=w1_scale[1][:, P * t : P * (t + 1)],
-                    rhs=xw1[s][:, r : r + CHUNK].bitcast(FP8X4),
+                    rhs=xw1[c].bitcast(FP8X4),
                     rhs_scale=xs[4:P, cols],
                     start=False,
                     stop=(t == PACK - 1),
@@ -197,51 +202,39 @@ def tile_picked_sub_mlp_gelu_sub_p_kernel(
                     nc.scalar.copy(yb[:, lo:hi], yb_bank[:, 0 : hi - lo])
             y.append(yb)
 
-        gt_bank = bank(7)
-        for c in range(VCH):
-            nc.tensor.transpose(gt_bank[:, P * c : P * (c + 1)], gate_rows[:, P * c : P * (c + 1)], ident[:])
-        gate_t = keep.tile([P, VCH, D], F32, name="gate_t")
-        nc.scalar.copy(gate_t[:], gt_bank[:, 0:V].rearrange("p (c r) -> p c r", c=VCH)[:, :, 0:D])
+        def term(d, b):
+            g = ring.tile([P, V], F32, name="picked")
+            nc.vector.tensor_tensor(g[:], y[b][:].indirect(pos_sb[d][:]), gate_sb[d][:], ALU.mult)
+            return g
 
-        turn_banks = ((6, 7), (0, 1))
-        out_bank = [bank(2 + b) for b in range(BLOCKS)]
-        last = D - 1
-        unit = 0
-        for pair in range(BLOCKS // 2):
-            blocks = (2 * pair, 2 * pair + 1)
-            turns = D if pair == 0 else D - 1
+        def summed(b, turns):
+            turned = bank((6, 7)[b % 2])
             for d in range(turns):
-                lo_bank, hi_bank = (bank(i) for i in turn_banks[unit % 2])
-                turned = [lo_bank[:, 0 : 2 * P], lo_bank[:, 2 * P : 4 * P], hi_bank[:, 0 : 2 * P]]
-                unit = unit + 1
-                for i, b in enumerate(blocks):
-                    g = ring.tile([P, V], F32, name="picked")
-                    nc.vector.tensor_copy(g[:], y[b][:].indirect(pos_sb[d][:]))
-                    for c in range(VCH):
-                        nc.tensor.transpose(turned[c][:, P * i : P * (i + 1)], g[:, P * c : P * (c + 1)], ident[:])
+                g = term(d, b)
                 for c in range(VCH):
-                    scaled = ring.tile([P, 2 * P], F32, name="scaled")
-                    nc.scalar.activation(scaled[:], turned[c], ACT.Copy, scale=gate_t[:, c, d : d + 1])
-                    for i, b in enumerate(blocks):
-                        nc.tensor.matmul(
-                            out_bank[b][:, P * c : P * (c + 1)],
-                            scaled[:, P * i : P * (i + 1)],
-                            ident[:],
-                            is_transpose=True,
-                            start=(d == 0 and c == 0),
-                            stop=(d == turns - 1 and c == VCH - 1),
-                        )
-            if pair == 0:
-                for b in blocks:
-                    res = keep.tile([P, V], F32, name="res%d" % b)
-                    nc.scalar.copy(res[:], out_bank[b][:, 0:V])
-                    nc.sync.dma_start(out=out[P * b : P * (b + 1), :], in_=res[:])
+                    nc.tensor.matmul(
+                        turned[:, P * c : P * (c + 1)],
+                        g[:, P * c : P * (c + 1)],
+                        ident[:],
+                        is_transpose=True,
+                        start=(d == 0 and c == 0),
+                        stop=(d == turns - 1 and c == VCH - 1),
+                    )
+            total = ring.tile([P, V], F32, name="total")
+            nc.scalar.copy(total[:], turned[:, 0:V])
+            back = bank((0, 1)[b % 2])
+            for c in range(VCH):
+                nc.tensor.transpose(back[:, P * c : P * (c + 1)], total[:, P * c : P * (c + 1)], ident[:])
+            return back
 
-        terms = {}
-        for b in range(BLOCKS - FUSED, BLOCKS):
-            terms[b] = ring.tile([P, V], F32, name="picked")
-            nc.vector.tensor_tensor(terms[b][:], y[b][:].indirect(pos_sb[last][:]), gate_last[:], ALU.mult)
-        for b in range(BLOCKS - FUSED, BLOCKS):
+        for b in range(BLOCKS - FUSED):
+            back = summed(b, D)
             res = keep.tile([P, V], F32, name="res%d" % b)
-            nc.vector.tensor_tensor(res[:], out_bank[b][:, 0:V], terms[b][:], ALU.add)
+            nc.scalar.copy(res[:], back[:, 0:V])
+            nc.sync.dma_start(out=out[P * b : P * (b + 1), :], in_=res[:])
+        backs = {b: summed(b, D - 1) for b in range(BLOCKS - FUSED, BLOCKS)}
+        terms = {b: term(D - 1, b) for b in backs}
+        for b in backs:
+            res = keep.tile([P, V], F32, name="res%d" % b)
+            nc.vector.tensor_tensor(res[:], backs[b][:, 0:V], terms[b][:], ALU.add)
             nc.sync.dma_start(out=out[P * b : P * (b + 1), :], in_=res[:])

@@ -27,10 +27,6 @@ BLOCKS = N // P
 VCH = V // P
 BANK = 512
 FUSED = 2
-CUTS = (
-    ((0, 256, "slot_bf00"), (256, 768, "slot_bf01")),
-    ((0, 256, "slot_bf10"), (256, 512, "slot_xall0"), (512, 768, "slot_w1raw1")),
-)
 
 
 def tile_picked_sub_mlp_gelu_sub_p_kernel(
@@ -45,25 +41,17 @@ def tile_picked_sub_mlp_gelu_sub_p_kernel(
         def bank(i):
             return psum.tile([P, BANK], F32, name="bank%d" % i, tag="bank%d" % i)
 
-        def slot(shape, dtype, name, tag):
-            return keep.tile(shape, dtype, name=name, tag=tag, align_bytes=64)
-
-        xs_all = slot([P, T], U8, "xs_all", "slot_scales")
+        xs_all = keep.tile([P, T], U8, name="xs_all", align_bytes=64)
         nc.gpsimd.memset(xs_all[:].bitcast(I32), 0)
-        for q in range(4):
-            nc.gpsimd.dma_start(
-                out=xs_all[32 * q : 32 * q + 4 * PASSES, :].bitcast(I32),
-                in_=x_scales[:, 4 * q : 4 * q + 4, :].bitcast(I32),
-            )
         warm = keep.tile([P, 1], F32, name="warm")
-        nc.vector.memset(warm[:], 0.0)
+        nc.gpsimd.memset(warm[:], 0.0)
         warm2 = keep.tile([P, 1], F32, name="warm2")
         nc.scalar.activation(warm2[:], warm[:], ACT.Gelu_apprx_tanh)
         ident = keep.tile([P, P], F32, name="ident")
         make_identity(nc, ident[:])
 
-        w1_raw = [slot([P, PACK, H], F32, "w1_raw%d" % o, "slot_w1raw%d" % o) for o in range(PASSES)]
-        xw_all = [slot([P, T], I32, "xw_all%d" % o, "slot_xall%d" % o) for o in range(PASSES)]
+        w1_raw = [keep.tile([P, PACK, H], F32, name="w1_raw%d" % o) for o in range(PASSES)]
+        xw_all = [keep.tile([P, T], I32, name="xw_all%d" % o, align_bytes=64) for o in range(PASSES)]
         offs_sb = keep.tile([P, S // 16], U16, name="offs_sb")
         for o in range(PASSES):
             nc.sync.dma_start(
@@ -71,6 +59,11 @@ def tile_picked_sub_mlp_gelu_sub_p_kernel(
             )
             if o == 0:
                 nc.sync.dma_start(offs_sb[:], offs)
+                for q in range(4):
+                    nc.sync.dma_start(
+                        out=xs_all[32 * q : 32 * q + 4 * PASSES, :].bitcast(I32),
+                        in_=x_scales[:, 4 * q : 4 * q + 4, :].bitcast(I32),
+                    )
             nc.sync.dma_start(out=xw_all[o][:], in_=x_words[o].rearrange("p c r -> p (c r)").bitcast(I32))
         w2_raw = keep.tile([P, PACK, N], F32, name="w2_raw")
         nc.sync.dma_start(out=w2_raw[:], in_=w2.rearrange("(p j) c -> p j c", j=PACK))
@@ -86,12 +79,12 @@ def tile_picked_sub_mlp_gelu_sub_p_kernel(
             gate_sb.append(t)
 
         w1_codes = [keep.tile([P, H], U32, name="w1_codes%d" % o, align_bytes=64) for o in range(PASSES)]
+        w1_scale = [keep.tile([P, H], U8, name="w1_scale%d" % o, align_bytes=64) for o in range(PASSES)]
 
         def w1_prepare(o):
             halves = []
             for u in range(2):
-                tag = "slot_xall0" if (o, u) == (1, 1) else "slot_bf%d%d" % (o, u)
-                g = slot([P, 2, P, PACK], BF16, "w1_bf%d%d" % (o, u), tag)
+                g = keep.tile([P, 2, P, PACK], BF16, name="w1_bf%d%d" % (o, u), align_bytes=64)
                 src = w1_raw[o][:].rearrange("p j (m t) -> p m j t", t=PACK)[:, :, :, 2 * u : 2 * u + 2]
                 dst = g[:].rearrange("p t m j -> p m j t")
                 if u == 0 or o == 0:
@@ -109,28 +102,29 @@ def tile_picked_sub_mlp_gelu_sub_p_kernel(
 
         def gather_words(o):
             slices = []
-            for s, (lo, hi, tag) in enumerate(CUTS[o]):
-                g = slot([P, hi - lo], U32, "xw%d_%d" % (o, s), tag)
-                nc.vector.tensor_copy(g[:], xw_all[o][:].bitcast(U32).indirect(offs_sb[:, lo // 16 : hi // 16]))
-                slices.extend(g[:, r : r + CHUNK] for r in range(0, hi - lo, CHUNK))
+            for s in range(S // SLICE):
+                g = keep.tile([P, SLICE], U32, name="xw%d_%d" % (o, s), align_bytes=64)
+                nc.vector.tensor_copy(
+                    g[:], xw_all[o][:].bitcast(U32).indirect(offs_sb[:, SLICE // 16 * s : SLICE // 16 * (s + 1)])
+                )
+                slices.append(g)
             return slices
 
         xs = keep.tile([P, S], U8, name="xs", align_bytes=64)
         nc.vector.tensor_copy(xs[:], xs_all[:].indirect(offs_sb[:]))
-        w1_scales = slot([P, PASSES * H], U8, "w1_scales", "slot_scales")
-        w1_scale = [w1_scales[:, H * o : H * (o + 1)] for o in range(PASSES)]
         w1_prepare(0)
         xw0 = gather_words(0)
 
         h_bank = [bank(c) for c in range(CHUNKS)]
         for c in range(CHUNKS):
             cols = slice(CHUNK * c, CHUNK * (c + 1))
+            s, r = divmod(CHUNK * c, SLICE)
             for t in range(PACK):
                 nc.tensor.matmul_mx(
                     out=h_bank[c][:, CHUNK * t : CHUNK * (t + 1)],
                     lhsT=w1_codes[0][:, P * t : P * (t + 1)].bitcast(FP8X4),
                     lhsT_scale=w1_scale[0][:, P * t : P * (t + 1)],
-                    rhs=xw0[c].bitcast(FP8X4),
+                    rhs=xw0[s][:, r : r + CHUNK].bitcast(FP8X4),
                     rhs_scale=xs[:, cols],
                     start=(t == 0),
                     stop=False,
@@ -145,27 +139,43 @@ def tile_picked_sub_mlp_gelu_sub_p_kernel(
         w2_codes = keep.tile([P, N], U32, name="w2_codes", align_bytes=64)
         w2_scale = keep.tile([P, N], U8, name="w2_scale", align_bytes=64)
 
-        def w2_prepare(u):
-            cols = slice(2 * P * u, 2 * P * (u + 1))
-            g = slot([P, 2 * P, PACK], BF16, "w2_bf%d" % u, ("slot_xall1", "slot_bf01")[u])
+        def w2_round(lo, hi):
+            g = keep.tile([P, hi - lo, PACK], BF16, name="w2_bf%d" % lo, align_bytes=64)
             nc.vector.tensor_copy(
                 g[:].rearrange("p (c i) j -> p c j i", i=4),
-                w2_raw[:, :, cols].rearrange("p j (c i) -> p c j i", i=4),
+                w2_raw[:, :, lo:hi].rearrange("p j (c i) -> p c j i", i=4),
             )
+            return g
+
+        def w2_quantize(g, lo, hi):
             nc.vector.quantize_mx(
-                out=w2_codes[:, cols].bitcast(FP8X4),
-                scales=w2_scale[:, cols],
+                out=w2_codes[:, lo:hi].bitcast(FP8X4),
+                scales=w2_scale[:, lo:hi],
                 in_=g[:].rearrange("p c j -> p (c j)"),
             )
 
+        def layer2(dst, b, lo, hi):
+            nc.tensor.matmul_mx(
+                out=dst,
+                lhsT=w2_codes[:, P * b : P * (b + 1)].bitcast(FP8X4),
+                lhsT_scale=w2_scale[:, P * b : P * (b + 1)],
+                rhs=h_codes[:, lo:hi].bitcast(FP8X4),
+                rhs_scale=h_scale[:, lo:hi],
+                start=True,
+                stop=True,
+            )
+
+        w2_parts = ((0, P), (P, 2 * P), (2 * P, N))
+        w2_bf = {}
         for c in range(CHUNKS):
             cols = slice(CHUNK * c, CHUNK * (c + 1))
+            s, r = divmod(CHUNK * c, SLICE)
             for t in range(PACK):
                 nc.tensor.matmul_mx(
                     out=h_bank[c][:, CHUNK * t : CHUNK * (t + 1)],
                     lhsT=w1_codes[1][:, P * t : P * (t + 1)].bitcast(FP8X4),
                     lhsT_scale=w1_scale[1][:, P * t : P * (t + 1)],
-                    rhs=xw1[c].bitcast(FP8X4),
+                    rhs=xw1[s][:, r : r + CHUNK].bitcast(FP8X4),
                     rhs_scale=xs[4:P, cols],
                     start=False,
                     stop=(t == PACK - 1),
@@ -180,27 +190,24 @@ def tile_picked_sub_mlp_gelu_sub_p_kernel(
                 in_=h_bf[:].rearrange("p n t -> p (n t)"),
             )
             if c in (1, 2):
-                w2_prepare(c - 1)
+                w2_quantize(w2_bf[c - 1], *w2_parts[c - 1])
+            if c < len(w2_parts):
+                w2_bf[c] = w2_round(*w2_parts[c])
+        w2_quantize(w2_bf[2], *w2_parts[2])
 
-        y = []
-        for b in range(BLOCKS):
-            yb = keep.tile([P, S], F32, name="y%d" % b)
+        y = [keep.tile([P, S], F32, name="y%d" % b) for b in range(BLOCKS)]
+        first = [bank(6), bank(7), bank(0)]
+        for c in range(CHUNKS):
+            dst = first[0][:, CHUNK * c : CHUNK * (c + 1)] if c < 4 else first[c - 3][:, 0:CHUNK]
+            layer2(dst, 0, CHUNK * c, CHUNK * (c + 1))
+        nc.scalar.copy(y[0][:, 0:BANK], first[0][:])
+        nc.scalar.copy(y[0][:, BANK : BANK + CHUNK], first[1][:, 0:CHUNK])
+        nc.vector.tensor_copy(y[0][:, BANK + CHUNK : S], first[2][:, 0:CHUNK])
+        for b in range(1, BLOCKS):
             for part, (lo, hi) in enumerate(((0, BANK), (BANK, S))):
-                yb_bank = bank((6 + 2 * b + part) % 8)
-                nc.tensor.matmul_mx(
-                    out=yb_bank[:, 0 : hi - lo],
-                    lhsT=w2_codes[:, P * b : P * (b + 1)].bitcast(FP8X4),
-                    lhsT_scale=w2_scale[:, P * b : P * (b + 1)],
-                    rhs=h_codes[:, lo:hi].bitcast(FP8X4),
-                    rhs_scale=h_scale[:, lo:hi],
-                    start=True,
-                    stop=True,
-                )
-                if b == 0 and part == 1:
-                    nc.vector.tensor_copy(yb[:, lo:hi], yb_bank[:, 0 : hi - lo])
-                else:
-                    nc.scalar.copy(yb[:, lo:hi], yb_bank[:, 0 : hi - lo])
-            y.append(yb)
+                yb_bank = bank(6 + part)
+                layer2(yb_bank[:, 0 : hi - lo], b, lo, hi)
+                nc.scalar.copy(y[b][:, lo:hi], yb_bank[:, 0 : hi - lo])
 
         def term(d, b):
             g = ring.tile([P, V], F32, name="picked")
@@ -208,7 +215,7 @@ def tile_picked_sub_mlp_gelu_sub_p_kernel(
             return g
 
         def summed(b, turns):
-            turned = bank((6, 7)[b % 2])
+            turned = bank((1, 2)[b % 2])
             for d in range(turns):
                 g = term(d, b)
                 for c in range(VCH):
@@ -222,7 +229,7 @@ def tile_picked_sub_mlp_gelu_sub_p_kernel(
                     )
             total = ring.tile([P, V], F32, name="total")
             nc.scalar.copy(total[:], turned[:, 0:V])
-            back = bank((0, 1)[b % 2])
+            back = bank((3, 4)[b % 2])
             for c in range(VCH):
                 nc.tensor.transpose(back[:, P * c : P * (c + 1)], total[:, P * c : P * (c + 1)], ident[:])
             return back

@@ -5,7 +5,7 @@ from concourse.masks import make_identity
 
 K, T, D, S, V, H, N = 1024, 2048, 4, 768, 384, 512, 512
 FLOPS = 2 * K * H * S + 2 * H * N * S
-BYTES = K * T + K * T // 32 + 4 * K * H + 4 * H * N + 4 * D * V + 2 * 8 * (S + D * V) + 4 * N * V
+BYTES = K * T + K * T // 32 + 4 * K * H + 4 * H * N + 4 * D * V + 16 * (S + D * V) + 4 * N * V
 
 F32 = mybir.dt.float32
 BF16 = mybir.dt.bfloat16
@@ -14,19 +14,29 @@ U32 = mybir.dt.uint32
 U16 = mybir.dt.uint16
 U8 = mybir.dt.uint8
 FP8X4 = mybir.dt.float8_e4m3fn_x4
-ACT = mybir.ActivationFunctionType
-ALU = mybir.AluOpType
+GELU = mybir.ActivationFunctionType.Gelu_apprx_tanh
+MULT = mybir.AluOpType.mult
+ADD = mybir.AluOpType.add
 
 P = 128
 PACK = 4
-PASSES = K // (P * PACK)
-CHUNK = 128
-CHUNKS = S // CHUNK
-SLICE = 256
-BLOCKS = N // P
-VCH = V // P
+PASS = P * PACK
+PASSES = K // PASS
+QUADRANTS = 4
+PER_COLUMN = 16
 BANK = 512
-FUSED = 2
+CHUNK = BANK // PACK
+CHUNKS = S // CHUNK
+SLICE = T // 8
+BLOCKS = N // P
+TURNS = V // P
+RING = 6
+W2_PARTS = ((0, P), (P, 2 * P), (2 * P, N))
+
+Y_BANKS = (6, 7)
+Y_LAST_BANK = 0
+SUM_BANKS = (1, 2)
+BACK_BANKS = (3, 4)
 
 
 def tile_picked_sub_mlp_gelu_sub_p_kernel(
@@ -35,213 +45,207 @@ def tile_picked_sub_mlp_gelu_sub_p_kernel(
     nc = tc.nc
     with ExitStack() as ctx:
         keep = ctx.enter_context(tc.tile_pool(name="keep", bufs=1))
-        ring = ctx.enter_context(tc.tile_pool(name="ring", bufs=6))
+        ring = ctx.enter_context(tc.tile_pool(name="ring", bufs=RING))
         psum = ctx.enter_context(tc.psum_pool(name="psum", bufs=1))
 
         def bank(i):
             return psum.tile([P, BANK], F32, name="bank%d" % i, tag="bank%d" % i)
 
-        xs_all = keep.tile([P, T], U8, name="xs_all", align_bytes=64)
-        nc.gpsimd.memset(xs_all[:].bitcast(I32), 0)
-        warm = keep.tile([P, 1], F32, name="warm")
-        nc.gpsimd.memset(warm[:], 0.0)
-        warm2 = keep.tile([P, 1], F32, name="warm2")
-        nc.scalar.activation(warm2[:], warm[:], ACT.Gelu_apprx_tanh)
-        ident = keep.tile([P, P], F32, name="ident")
-        make_identity(nc, ident[:])
+        def quantize(codes, scales, rounded):
+            nc.vector.quantize_mx(out=codes.bitcast(FP8X4), scales=scales, in_=rounded)
 
-        w1_raw = [keep.tile([P, PACK, H], F32, name="w1_raw%d" % o) for o in range(PASSES)]
-        xw_all = [keep.tile([P, T], I32, name="xw_all%d" % o, align_bytes=64) for o in range(PASSES)]
-        offs_sb = keep.tile([P, S // 16], U16, name="offs_sb")
-        for o in range(PASSES):
-            nc.sync.dma_start(
-                out=w1_raw[o][:], in_=w1[512 * o : 512 * (o + 1), :].rearrange("(p j) c -> p j c", j=PACK)
-            )
-            if o == 0:
-                nc.sync.dma_start(offs_sb[:], offs)
-                for q in range(4):
-                    nc.sync.dma_start(
-                        out=xs_all[32 * q : 32 * q + 4 * PASSES, :].bitcast(I32),
-                        in_=x_scales[:, 4 * q : 4 * q + 4, :].bitcast(I32),
-                    )
-            nc.sync.dma_start(out=xw_all[o][:], in_=x_words[o].rearrange("p c r -> p (c r)").bitcast(I32))
-        w2_raw = keep.tile([P, PACK, N], F32, name="w2_raw")
-        nc.sync.dma_start(out=w2_raw[:], in_=w2.rearrange("(p j) c -> p j c", j=PACK))
-        pos_sb = []
-        for d, pos in enumerate((pos1, pos2, pos3, pos4)):
-            t = keep.tile([P, V // 16], U16, name="pos_sb%d" % d)
-            nc.sync.dma_start(t[:], pos)
-            pos_sb.append(t)
-        gate_sb = []
-        for d in range(D):
-            t = keep.tile([P, V], F32, name="gate_sb%d" % d)
-            nc.sync.dma_start(out=t[:], in_=gate[d, 0:P, :])
-            gate_sb.append(t)
-
-        w1_codes = [keep.tile([P, H], U32, name="w1_codes%d" % o, align_bytes=64) for o in range(PASSES)]
-        w1_scale = [keep.tile([P, H], U8, name="w1_scale%d" % o, align_bytes=64) for o in range(PASSES)]
-
-        def w1_prepare(o):
-            halves = []
-            for u in range(2):
-                g = keep.tile([P, 2, P, PACK], BF16, name="w1_bf%d%d" % (o, u), align_bytes=64)
-                src = w1_raw[o][:].rearrange("p j (m t) -> p m j t", t=PACK)[:, :, :, 2 * u : 2 * u + 2]
-                dst = g[:].rearrange("p t m j -> p m j t")
-                if u == 0 or o == 0:
-                    nc.scalar.copy(dst, src)
-                else:
-                    nc.vector.tensor_copy(dst, src)
-                halves.append(g)
-            for u in ((0, 1), (1, 0))[o]:
-                cols = slice(2 * P * u, 2 * P * (u + 1))
-                nc.vector.quantize_mx(
-                    out=w1_codes[o][:, cols].bitcast(FP8X4),
-                    scales=w1_scale[o][:, cols],
-                    in_=halves[u][:].rearrange("p t m j -> p (t m j)"),
-                )
-
-        def gather_words(o):
-            slices = []
-            for s in range(S // SLICE):
-                g = keep.tile([P, SLICE], U32, name="xw%d_%d" % (o, s), align_bytes=64)
-                nc.vector.tensor_copy(
-                    g[:], xw_all[o][:].bitcast(U32).indirect(offs_sb[:, SLICE // 16 * s : SLICE // 16 * (s + 1)])
-                )
-                slices.append(g)
-            return slices
-
-        xs = keep.tile([P, S], U8, name="xs", align_bytes=64)
-        nc.vector.tensor_copy(xs[:], xs_all[:].indirect(offs_sb[:]))
-        w1_prepare(0)
-        xw0 = gather_words(0)
-
-        h_bank = [bank(c) for c in range(CHUNKS)]
-        for c in range(CHUNKS):
-            cols = slice(CHUNK * c, CHUNK * (c + 1))
-            s, r = divmod(CHUNK * c, SLICE)
-            for t in range(PACK):
-                nc.tensor.matmul_mx(
-                    out=h_bank[c][:, CHUNK * t : CHUNK * (t + 1)],
-                    lhsT=w1_codes[0][:, P * t : P * (t + 1)].bitcast(FP8X4),
-                    lhsT_scale=w1_scale[0][:, P * t : P * (t + 1)],
-                    rhs=xw0[s][:, r : r + CHUNK].bitcast(FP8X4),
-                    rhs_scale=xs[:, cols],
-                    start=(t == 0),
-                    stop=False,
-                )
-
-        w1_prepare(1)
-
-        xw1 = gather_words(1)
-
-        h_codes = keep.tile([P, S], U32, name="h_codes", align_bytes=64)
-        h_scale = keep.tile([P, S], U8, name="h_scale", align_bytes=64)
-        w2_codes = keep.tile([P, N], U32, name="w2_codes", align_bytes=64)
-        w2_scale = keep.tile([P, N], U8, name="w2_scale", align_bytes=64)
-
-        def w2_round(lo, hi):
-            g = keep.tile([P, hi - lo, PACK], BF16, name="w2_bf%d" % lo, align_bytes=64)
-            nc.vector.tensor_copy(
-                g[:].rearrange("p (c i) j -> p c j i", i=4),
-                w2_raw[:, :, lo:hi].rearrange("p j (c i) -> p c j i", i=4),
-            )
-            return g
-
-        def w2_quantize(g, lo, hi):
-            nc.vector.quantize_mx(
-                out=w2_codes[:, lo:hi].bitcast(FP8X4),
-                scales=w2_scale[:, lo:hi],
-                in_=g[:].rearrange("p c j -> p (c j)"),
-            )
-
-        def layer2(dst, b, lo, hi):
+        def product(dst, w_codes, w_scales, codes, scales, start, stop):
             nc.tensor.matmul_mx(
                 out=dst,
-                lhsT=w2_codes[:, P * b : P * (b + 1)].bitcast(FP8X4),
-                lhsT_scale=w2_scale[:, P * b : P * (b + 1)],
-                rhs=h_codes[:, lo:hi].bitcast(FP8X4),
-                rhs_scale=h_scale[:, lo:hi],
-                start=True,
-                stop=True,
+                lhsT=w_codes.bitcast(FP8X4),
+                lhsT_scale=w_scales,
+                rhs=codes.bitcast(FP8X4),
+                rhs_scale=scales,
+                start=start,
+                stop=stop,
             )
 
-        w2_parts = ((0, P), (P, 2 * P), (2 * P, N))
-        w2_bf = {}
+        scales_all = keep.tile([P, T], U8, name="scales_all", align_bytes=64)
+        nc.vector.memset(scales_all[:].bitcast(I32), 0)
+        ident = keep.tile([P, P], F32, name="ident")
+        make_identity(nc, ident[:])
+        warm = keep.tile([P, 1], F32, name="warm")
+        nc.scalar.activation(warm[:], ident[:, 0:1], GELU)
+
+        words_all = [keep.tile([P, T], I32, name="words_all%d" % o, align_bytes=64) for o in range(PASSES)]
+        w1_raw = [keep.tile([P, PACK, H], F32, name="w1_raw%d" % o) for o in range(PASSES)]
+        w2_raw = keep.tile([P, PACK, N], F32, name="w2_raw")
+        offs_sb = keep.tile([P, S // PER_COLUMN], U16, name="offs_sb")
+        pos_sb = [keep.tile([P, V // PER_COLUMN], U16, name="pos_sb%d" % d) for d in range(D)]
+        gate_sb = [keep.tile([P, V], F32, name="gate_sb%d" % d) for d in range(D)]
+
+        def load_words(o):
+            nc.sync.dma_start(out=words_all[o][:], in_=x_words[o].rearrange("p c r -> p (c r)").bitcast(I32))
+
+        def load_rows(dst, rows):
+            nc.sync.dma_start(out=dst[:], in_=rows.rearrange("(p j) c -> p j c", j=PACK))
+
+        load_words(0)
+        nc.sync.dma_start(offs_sb[:], offs)
+        for q in range(QUADRANTS):
+            nc.sync.dma_start(
+                out=scales_all[32 * q : 32 * q + 4 * PASSES, :].bitcast(I32),
+                in_=x_scales[:, 4 * q : 4 * q + 4, :].bitcast(I32),
+            )
+        for o in range(PASSES):
+            load_rows(w1_raw[o], w1[PASS * o : PASS * (o + 1), :])
+        load_words(1)
+        load_rows(w2_raw, w2)
+        for dst, pos in zip(pos_sb, (pos1, pos2, pos3, pos4)):
+            nc.sync.dma_start(dst[:], pos)
+        for d in range(D):
+            nc.sync.dma_start(out=gate_sb[d][:], in_=gate[d, 0:P, :])
+
+        w1_codes = [keep.tile([P, H], U32, name="w1_codes%d" % o, align_bytes=64) for o in range(PASSES)]
+        w1_scales = [keep.tile([P, H], U8, name="w1_scales%d" % o, align_bytes=64) for o in range(PASSES)]
+
+        def w1_round(o, u, copy):
+            rounded = keep.tile([P, 2, P, PACK], BF16, name="w1_bf%d%d" % (o, u), align_bytes=64)
+            src = w1_raw[o][:].rearrange("p j (m t) -> p m j t", t=PACK)[:, :, :, 2 * u : 2 * u + 2]
+            copy(rounded[:].rearrange("p t m j -> p m j t"), src)
+            return rounded
+
+        def w1_quantize(o, u, rounded):
+            cols = slice(2 * P * u, 2 * P * (u + 1))
+            quantize(w1_codes[o][:, cols], w1_scales[o][:, cols], rounded[:].rearrange("p t m j -> p (t m j)"))
+
+        words0 = keep.tile([P, S], U32, name="words0", align_bytes=64)
+        nc.vector.tensor_copy(words0[:], words_all[0][:].bitcast(U32).indirect(offs_sb[:]))
+        scales = keep.tile([P, S], U8, name="scales", align_bytes=64)
+        nc.vector.tensor_copy(scales[:], scales_all[:].indirect(offs_sb[:]))
+
+        halves = [w1_round(0, u, nc.scalar.copy) for u in range(2)]
+        for u in range(2):
+            w1_quantize(0, u, halves[u])
+
+        h_bank = [bank(c) for c in range(CHUNKS)]
+
+        def layer1(o, c, t, words):
+            product(
+                h_bank[c][:, CHUNK * t : CHUNK * (t + 1)],
+                w1_codes[o][:, P * t : P * (t + 1)],
+                w1_scales[o][:, P * t : P * (t + 1)],
+                words,
+                scales[4 * o : P, CHUNK * c : CHUNK * (c + 1)],
+                start=(o == 0 and t == 0),
+                stop=(o == PASSES - 1 and t == PACK - 1),
+            )
+
+        for t in range(PACK):
+            for c in range(CHUNKS):
+                layer1(0, c, t, words0[:, CHUNK * c : CHUNK * (c + 1)])
+
+        halves = [w1_round(1, 0, nc.scalar.copy), w1_round(1, 1, nc.vector.tensor_copy)]
+        for u in (1, 0):
+            w1_quantize(1, u, halves[u])
+
+        words1 = []
+        for lo in range(0, S, SLICE):
+            picked = keep.tile([P, SLICE], U32, name="words1_%d" % lo, align_bytes=64)
+            entries = offs_sb[:, lo // PER_COLUMN : (lo + SLICE) // PER_COLUMN]
+            nc.vector.tensor_copy(picked[:], words_all[1][:].bitcast(U32).indirect(entries))
+            words1.extend(picked[:, r : r + CHUNK] for r in range(0, SLICE, CHUNK))
+
+        h_codes = keep.tile([P, S], U32, name="h_codes", align_bytes=64)
+        h_scales = keep.tile([P, S], U8, name="h_scales", align_bytes=64)
+        w2_codes = keep.tile([P, N], U32, name="w2_codes", align_bytes=64)
+        w2_scales = keep.tile([P, N], U8, name="w2_scales", align_bytes=64)
+
+        def w2_round(lo, hi):
+            rounded = keep.tile([P, hi - lo, PACK], BF16, name="w2_bf%d" % lo, align_bytes=64)
+            nc.vector.tensor_copy(
+                rounded[:].rearrange("p (c i) j -> p c j i", i=4),
+                w2_raw[:, :, lo:hi].rearrange("p j (c i) -> p c j i", i=4),
+            )
+            return rounded
+
+        def w2_quantize(part, rounded):
+            lo, hi = W2_PARTS[part]
+            quantize(w2_codes[:, lo:hi], w2_scales[:, lo:hi], rounded[:].rearrange("p c j -> p (c j)"))
+
+        last_part = len(W2_PARTS) - 1
+        w2_bf = []
         for c in range(CHUNKS):
             cols = slice(CHUNK * c, CHUNK * (c + 1))
-            s, r = divmod(CHUNK * c, SLICE)
             for t in range(PACK):
-                nc.tensor.matmul_mx(
-                    out=h_bank[c][:, CHUNK * t : CHUNK * (t + 1)],
-                    lhsT=w1_codes[1][:, P * t : P * (t + 1)].bitcast(FP8X4),
-                    lhsT_scale=w1_scale[1][:, P * t : P * (t + 1)],
-                    rhs=xw1[s][:, r : r + CHUNK].bitcast(FP8X4),
-                    rhs_scale=xs[4:P, cols],
-                    start=False,
-                    stop=(t == PACK - 1),
-                )
+                layer1(1, c, t, words1[c])
             h_bf = keep.tile([P, CHUNK, PACK], BF16, name="h_bf%d" % c, align_bytes=64)
-            nc.scalar.activation(
-                h_bf[:], h_bank[c][:].rearrange("p (t n) -> p n t", t=PACK), ACT.Gelu_apprx_tanh
-            )
-            nc.vector.quantize_mx(
-                out=h_codes[:, cols].bitcast(FP8X4),
-                scales=h_scale[:, cols],
-                in_=h_bf[:].rearrange("p n t -> p (n t)"),
-            )
-            if c in (1, 2):
-                w2_quantize(w2_bf[c - 1], *w2_parts[c - 1])
-            if c < len(w2_parts):
-                w2_bf[c] = w2_round(*w2_parts[c])
-        w2_quantize(w2_bf[2], *w2_parts[2])
+            nc.scalar.activation(h_bf[:], h_bank[c][:].rearrange("p (t n) -> p n t", t=PACK), GELU)
+            quantize(h_codes[:, cols], h_scales[:, cols], h_bf[:].rearrange("p n t -> p (n t)"))
+            if 1 <= c <= last_part:
+                w2_quantize(c - 1, w2_bf[c - 1])
+            if c <= last_part:
+                w2_bf.append(w2_round(*W2_PARTS[c]))
+        w2_quantize(last_part, w2_bf[last_part])
+
+        def layer2(dst, b, lo, hi):
+            rows = slice(P * b, P * (b + 1))
+            product(dst, w2_codes[:, rows], w2_scales[:, rows], h_codes[:, lo:hi], h_scales[:, lo:hi], True, True)
 
         y = [keep.tile([P, S], F32, name="y%d" % b) for b in range(BLOCKS)]
-        first = [bank(6), bank(7), bank(0)]
-        for c in range(CHUNKS):
-            dst = first[0][:, CHUNK * c : CHUNK * (c + 1)] if c < 4 else first[c - 3][:, 0:CHUNK]
-            layer2(dst, 0, CHUNK * c, CHUNK * (c + 1))
-        nc.scalar.copy(y[0][:, 0:BANK], first[0][:])
-        nc.scalar.copy(y[0][:, BANK : BANK + CHUNK], first[1][:, 0:CHUNK])
-        nc.vector.tensor_copy(y[0][:, BANK + CHUNK : S], first[2][:, 0:CHUNK])
+        wide, single, closing = bank(Y_BANKS[0]), bank(Y_BANKS[1]), bank(Y_LAST_BANK)
+        for lo in range(0, BANK, CHUNK):
+            layer2(wide[:, lo : lo + CHUNK], 0, lo, lo + CHUNK)
+        layer2(single[:, 0:CHUNK], 0, BANK, BANK + CHUNK)
+        layer2(closing[:, 0:CHUNK], 0, BANK + CHUNK, S)
+        nc.scalar.copy(y[0][:, 0:BANK], wide[:])
+        nc.scalar.copy(y[0][:, BANK : BANK + CHUNK], single[:, 0:CHUNK])
+        nc.vector.tensor_copy(y[0][:, BANK + CHUNK : S], closing[:, 0:CHUNK])
         for b in range(1, BLOCKS):
-            for part, (lo, hi) in enumerate(((0, BANK), (BANK, S))):
-                yb_bank = bank(6 + part)
-                layer2(yb_bank[:, 0 : hi - lo], b, lo, hi)
-                nc.scalar.copy(y[b][:, lo:hi], yb_bank[:, 0 : hi - lo])
+            for i, (lo, hi) in zip(Y_BANKS, ((0, BANK), (BANK, S))):
+                acc = bank(i)
+                layer2(acc[:, 0 : hi - lo], b, lo, hi)
+                nc.scalar.copy(y[b][:, lo:hi], acc[:, 0 : hi - lo])
 
-        def term(d, b):
-            g = ring.tile([P, V], F32, name="picked")
-            nc.vector.tensor_tensor(g[:], y[b][:].indirect(pos_sb[d][:]), gate_sb[d][:], ALU.mult)
-            return g
+        def term(d, b, lo, hi):
+            made = ring.tile([P, hi - lo], F32, name="term")
+            entries = pos_sb[d][:, lo // PER_COLUMN : hi // PER_COLUMN]
+            nc.vector.tensor_tensor(made[:], y[b][:].indirect(entries), gate_sb[d][:, lo:hi], MULT)
+            return made
 
-        def summed(b, turns):
-            turned = bank((1, 2)[b % 2])
-            for d in range(turns):
-                g = term(d, b)
-                for c in range(VCH):
+        def summed(b, count):
+            turned = bank(SUM_BANKS[b % 2])
+            for d in range(count):
+                made = term(d, b, 0, V)
+                for c in range(TURNS):
                     nc.tensor.matmul(
                         turned[:, P * c : P * (c + 1)],
-                        g[:, P * c : P * (c + 1)],
+                        made[:, P * c : P * (c + 1)],
                         ident[:],
                         is_transpose=True,
                         start=(d == 0 and c == 0),
-                        stop=(d == turns - 1 and c == VCH - 1),
+                        stop=(d == count - 1 and c == TURNS - 1),
                     )
             total = ring.tile([P, V], F32, name="total")
             nc.scalar.copy(total[:], turned[:, 0:V])
-            back = bank((3, 4)[b % 2])
-            for c in range(VCH):
+            back = bank(BACK_BANKS[b % 2])
+            for c in range(TURNS):
                 nc.tensor.transpose(back[:, P * c : P * (c + 1)], total[:, P * c : P * (c + 1)], ident[:])
             return back
 
-        for b in range(BLOCKS - FUSED):
+        def add_and_store(b, lo, hi, back, made):
+            result = keep.tile([P, hi - lo], F32, name="result%d_%d" % (b, lo))
+            nc.vector.tensor_tensor(result[:], back[:, lo:hi], made[:], ADD)
+            nc.sync.dma_start(out=out[P * b : P * (b + 1), lo:hi], in_=result[:])
+
+        for b in range(BLOCKS - 2):
             back = summed(b, D)
-            res = keep.tile([P, V], F32, name="res%d" % b)
-            nc.scalar.copy(res[:], back[:, 0:V])
-            nc.sync.dma_start(out=out[P * b : P * (b + 1), :], in_=res[:])
-        backs = {b: summed(b, D - 1) for b in range(BLOCKS - FUSED, BLOCKS)}
-        terms = {b: term(D - 1, b) for b in backs}
-        for b in backs:
-            res = keep.tile([P, V], F32, name="res%d" % b)
-            nc.vector.tensor_tensor(res[:], backs[b][:, 0:V], terms[b][:], ALU.add)
-            nc.sync.dma_start(out=out[P * b : P * (b + 1), :], in_=res[:])
+            result = keep.tile([P, V], F32, name="result%d" % b)
+            nc.scalar.copy(result[:], back[:, 0:V])
+            nc.sync.dma_start(out=out[P * b : P * (b + 1), :], in_=result[:])
+
+        second, final = BLOCKS - 2, BLOCKS - 1
+        half = V // 2
+        back_second = summed(second, D - 1)
+        back_final = summed(final, D - 1)
+        term_second = term(D - 1, second, 0, V)
+        term_low = term(D - 1, final, 0, half)
+        add_and_store(second, 0, V, back_second, term_second)
+        term_high = term(D - 1, final, half, V)
+        add_and_store(final, 0, half, back_final, term_low)
+        add_and_store(final, half, V, back_final, term_high)

from contextlib import ExitStack

import concourse.mybir as mybir
from concourse.masks import make_identity

K, T, D, S, V, H, N = 1024, 2048, 4, 768, 384, 512, 512
FLOPS = 2 * K * H * S + 2 * H * N * S
BYTES = K * T + K * T // 32 + 4 * K * H + 4 * H * N + 4 * D * V + 16 * (S + D * V) + 4 * N * V

F32 = mybir.dt.float32
BF16 = mybir.dt.bfloat16
I32 = mybir.dt.int32
U32 = mybir.dt.uint32
U16 = mybir.dt.uint16
U8 = mybir.dt.uint8
FP8X4 = mybir.dt.float8_e4m3fn_x4
GELU = mybir.ActivationFunctionType.Gelu_apprx_tanh
MULT = mybir.AluOpType.mult
ADD = mybir.AluOpType.add

P = 128
PACK = 4
PASS = P * PACK
PASSES = K // PASS
QUADRANTS = 4
PER_COLUMN = 16
BANK = 512
CHUNK = BANK // PACK
CHUNKS = S // CHUNK
SLICE = T // 8
BLOCKS = N // P
TURNS = V // P
RING = 6
W2_PARTS = ((0, P), (P, 2 * P), (2 * P, N))

Y_BANKS = (6, 7)
Y_LAST_BANK = 0
SUM_BANKS = (1, 2)
BACK_BANKS = (3, 4)


def tile_picked_sub_mlp_gelu_sub_p_kernel(
    tc, x_words, x_scales, w1, w2, gate, offs, pos1, pos2, pos3, pos4, out
):
    nc = tc.nc
    with ExitStack() as ctx:
        keep = ctx.enter_context(tc.tile_pool(name="keep", bufs=1))
        ring = ctx.enter_context(tc.tile_pool(name="ring", bufs=RING))
        psum = ctx.enter_context(tc.psum_pool(name="psum", bufs=1))

        def bank(i):
            return psum.tile([P, BANK], F32, name="bank%d" % i, tag="bank%d" % i)

        def quantize(codes, scales, rounded):
            nc.vector.quantize_mx(out=codes.bitcast(FP8X4), scales=scales, in_=rounded)

        def product(dst, w_codes, w_scales, codes, scales, start, stop):
            nc.tensor.matmul_mx(
                out=dst,
                lhsT=w_codes.bitcast(FP8X4),
                lhsT_scale=w_scales,
                rhs=codes.bitcast(FP8X4),
                rhs_scale=scales,
                start=start,
                stop=stop,
            )

        scales_all = keep.tile([P, T], U8, name="scales_all", align_bytes=64)
        nc.vector.memset(scales_all[:].bitcast(I32), 0)
        ident = keep.tile([P, P], F32, name="ident")
        make_identity(nc, ident[:])
        warm = keep.tile([P, 1], F32, name="warm")
        nc.scalar.activation(warm[:], ident[:, 0:1], GELU)

        words_all = [keep.tile([P, T], I32, name="words_all%d" % o, align_bytes=64) for o in range(PASSES)]
        w1_raw = [keep.tile([P, PACK, H], F32, name="w1_raw%d" % o) for o in range(PASSES)]
        w2_raw = keep.tile([P, PACK, N], F32, name="w2_raw")
        offs_sb = keep.tile([P, S // PER_COLUMN], U16, name="offs_sb")
        pos_sb = [keep.tile([P, V // PER_COLUMN], U16, name="pos_sb%d" % d) for d in range(D)]
        gate_sb = [keep.tile([P, V], F32, name="gate_sb%d" % d) for d in range(D)]

        def load_words(o):
            nc.sync.dma_start(out=words_all[o][:], in_=x_words[o].rearrange("p c r -> p (c r)").bitcast(I32))

        def load_rows(dst, rows):
            nc.sync.dma_start(out=dst[:], in_=rows.rearrange("(p j) c -> p j c", j=PACK))

        load_words(0)
        nc.sync.dma_start(offs_sb[:], offs)
        for q in range(QUADRANTS):
            nc.sync.dma_start(
                out=scales_all[32 * q : 32 * q + 4 * PASSES, :].bitcast(I32),
                in_=x_scales[:, 4 * q : 4 * q + 4, :].bitcast(I32),
            )
        for o in range(PASSES):
            load_rows(w1_raw[o], w1[PASS * o : PASS * (o + 1), :])
        load_words(1)
        load_rows(w2_raw, w2)
        for dst, pos in zip(pos_sb, (pos1, pos2, pos3, pos4)):
            nc.sync.dma_start(dst[:], pos)
        for d in range(D):
            nc.sync.dma_start(out=gate_sb[d][:], in_=gate[d, 0:P, :])

        w1_codes = [keep.tile([P, H], U32, name="w1_codes%d" % o, align_bytes=64) for o in range(PASSES)]
        w1_scales = [keep.tile([P, H], U8, name="w1_scales%d" % o, align_bytes=64) for o in range(PASSES)]

        def w1_round(o, u, copy):
            rounded = keep.tile([P, 2, P, PACK], BF16, name="w1_bf%d%d" % (o, u), align_bytes=64)
            src = w1_raw[o][:].rearrange("p j (m t) -> p m j t", t=PACK)[:, :, :, 2 * u : 2 * u + 2]
            copy(rounded[:].rearrange("p t m j -> p m j t"), src)
            return rounded

        def w1_quantize(o, u, rounded):
            cols = slice(2 * P * u, 2 * P * (u + 1))
            quantize(w1_codes[o][:, cols], w1_scales[o][:, cols], rounded[:].rearrange("p t m j -> p (t m j)"))

        words0 = keep.tile([P, S], U32, name="words0", align_bytes=64)
        nc.vector.tensor_copy(words0[:], words_all[0][:].bitcast(U32).indirect(offs_sb[:]))
        scales = keep.tile([P, S], U8, name="scales", align_bytes=64)
        nc.vector.tensor_copy(scales[:], scales_all[:].indirect(offs_sb[:]))

        halves = [w1_round(0, u, nc.scalar.copy) for u in range(2)]
        for u in range(2):
            w1_quantize(0, u, halves[u])

        h_bank = [bank(c) for c in range(CHUNKS)]

        def layer1(o, c, t, words):
            product(
                h_bank[c][:, CHUNK * t : CHUNK * (t + 1)],
                w1_codes[o][:, P * t : P * (t + 1)],
                w1_scales[o][:, P * t : P * (t + 1)],
                words,
                scales[4 * o : P, CHUNK * c : CHUNK * (c + 1)],
                start=(o == 0 and t == 0),
                stop=(o == PASSES - 1 and t == PACK - 1),
            )

        for t in range(PACK):
            for c in range(CHUNKS):
                layer1(0, c, t, words0[:, CHUNK * c : CHUNK * (c + 1)])

        halves = [w1_round(1, 0, nc.scalar.copy), w1_round(1, 1, nc.vector.tensor_copy)]
        for u in (1, 0):
            w1_quantize(1, u, halves[u])

        words1 = []
        for lo in range(0, S, SLICE):
            picked = keep.tile([P, SLICE], U32, name="words1_%d" % lo, align_bytes=64)
            entries = offs_sb[:, lo // PER_COLUMN : (lo + SLICE) // PER_COLUMN]
            nc.vector.tensor_copy(picked[:], words_all[1][:].bitcast(U32).indirect(entries))
            words1.extend(picked[:, r : r + CHUNK] for r in range(0, SLICE, CHUNK))

        h_codes = keep.tile([P, S], U32, name="h_codes", align_bytes=64)
        h_scales = keep.tile([P, S], U8, name="h_scales", align_bytes=64)
        w2_codes = keep.tile([P, N], U32, name="w2_codes", align_bytes=64)
        w2_scales = keep.tile([P, N], U8, name="w2_scales", align_bytes=64)

        def w2_round(lo, hi):
            rounded = keep.tile([P, hi - lo, PACK], BF16, name="w2_bf%d" % lo, align_bytes=64)
            nc.vector.tensor_copy(
                rounded[:].rearrange("p (c i) j -> p c j i", i=4),
                w2_raw[:, :, lo:hi].rearrange("p j (c i) -> p c j i", i=4),
            )
            return rounded

        def w2_quantize(part, rounded):
            lo, hi = W2_PARTS[part]
            quantize(w2_codes[:, lo:hi], w2_scales[:, lo:hi], rounded[:].rearrange("p c j -> p (c j)"))

        last_part = len(W2_PARTS) - 1
        w2_bf = []
        for c in range(CHUNKS):
            cols = slice(CHUNK * c, CHUNK * (c + 1))
            for t in range(PACK):
                layer1(1, c, t, words1[c])
            h_bf = keep.tile([P, CHUNK, PACK], BF16, name="h_bf%d" % c, align_bytes=64)
            nc.scalar.activation(h_bf[:], h_bank[c][:].rearrange("p (t n) -> p n t", t=PACK), GELU)
            quantize(h_codes[:, cols], h_scales[:, cols], h_bf[:].rearrange("p n t -> p (n t)"))
            if 1 <= c <= last_part:
                w2_quantize(c - 1, w2_bf[c - 1])
            if c <= last_part:
                w2_bf.append(w2_round(*W2_PARTS[c]))
        w2_quantize(last_part, w2_bf[last_part])

        def layer2(dst, b, lo, hi):
            rows = slice(P * b, P * (b + 1))
            product(dst, w2_codes[:, rows], w2_scales[:, rows], h_codes[:, lo:hi], h_scales[:, lo:hi], True, True)

        y = [keep.tile([P, S], F32, name="y%d" % b) for b in range(BLOCKS)]
        wide, single, closing = bank(Y_BANKS[0]), bank(Y_BANKS[1]), bank(Y_LAST_BANK)
        for lo in range(0, BANK, CHUNK):
            layer2(wide[:, lo : lo + CHUNK], 0, lo, lo + CHUNK)
        layer2(single[:, 0:CHUNK], 0, BANK, BANK + CHUNK)
        layer2(closing[:, 0:CHUNK], 0, BANK + CHUNK, S)
        nc.scalar.copy(y[0][:, 0:BANK], wide[:])
        nc.scalar.copy(y[0][:, BANK : BANK + CHUNK], single[:, 0:CHUNK])
        nc.vector.tensor_copy(y[0][:, BANK + CHUNK : S], closing[:, 0:CHUNK])
        for b in range(1, BLOCKS):
            for i, (lo, hi) in zip(Y_BANKS, ((0, BANK), (BANK, S))):
                acc = bank(i)
                layer2(acc[:, 0 : hi - lo], b, lo, hi)
                nc.scalar.copy(y[b][:, lo:hi], acc[:, 0 : hi - lo])

        def term(d, b, lo, hi):
            made = ring.tile([P, hi - lo], F32, name="term")
            entries = pos_sb[d][:, lo // PER_COLUMN : hi // PER_COLUMN]
            nc.vector.tensor_tensor(made[:], y[b][:].indirect(entries), gate_sb[d][:, lo:hi], MULT)
            return made

        def summed(b, count):
            turned = bank(SUM_BANKS[b % 2])
            for d in range(count):
                made = term(d, b, 0, V)
                for c in range(TURNS):
                    nc.tensor.matmul(
                        turned[:, P * c : P * (c + 1)],
                        made[:, P * c : P * (c + 1)],
                        ident[:],
                        is_transpose=True,
                        start=(d == 0 and c == 0),
                        stop=(d == count - 1 and c == TURNS - 1),
                    )
            total = ring.tile([P, V], F32, name="total")
            nc.scalar.copy(total[:], turned[:, 0:V])
            back = bank(BACK_BANKS[b % 2])
            for c in range(TURNS):
                nc.tensor.transpose(back[:, P * c : P * (c + 1)], total[:, P * c : P * (c + 1)], ident[:])
            return back

        def add_and_store(b, lo, hi, back, made):
            result = keep.tile([P, hi - lo], F32, name="result%d_%d" % (b, lo))
            nc.vector.tensor_tensor(result[:], back[:, lo:hi], made[:], ADD)
            nc.sync.dma_start(out=out[P * b : P * (b + 1), lo:hi], in_=result[:])

        for b in range(BLOCKS - 2):
            back = summed(b, D)
            result = keep.tile([P, V], F32, name="result%d" % b)
            nc.scalar.copy(result[:], back[:, 0:V])
            nc.sync.dma_start(out=out[P * b : P * (b + 1), :], in_=result[:])

        second, final = BLOCKS - 2, BLOCKS - 1
        half = V // 2
        back_second = summed(second, D - 1)
        back_final = summed(final, D - 1)
        term_second = term(D - 1, second, 0, V)
        term_low = term(D - 1, final, 0, half)
        add_and_store(second, 0, V, back_second, term_second)
        term_high = term(D - 1, final, half, V)
        add_and_store(final, 0, half, back_final, term_low)
        add_and_store(final, half, V, back_final, term_high)
